import numpy as np, ml_dtypes
CORES = [36,164,52,180,100,228,116,244]
N = 8
BF = ml_dtypes.bfloat16
def gentries(a):
    return np.ascontiguousarray(a.reshape(8, 16, -1).transpose(0, 2, 1)).reshape(8, -1)
def gtable(e):
    e = np.asarray(e); return np.ascontiguousarray(e.reshape(8, -1, 16).transpose(0, 2, 1)).reshape(128, -1).astype(np.int32)
V, D, L, CAP, RO = 2048, 4, 6, 192, 2
K = V // 256
def pack(w, z, cd):
    return {"wish": np.ascontiguousarray(w.reshape(N, 128, V)).astype(np.float32).astype(BF), "goods": np.ascontiguousarray(z.reshape(N, 128, V)).astype(np.float32).astype(BF),
            "cand": np.stack([gtable(a.reshape(8, -1)) for a in cd])}
def ring(o, m):
    a = o[:len(o) // m * m].reshape(-1, m)
    return a, np.roll(a, -1, axis=1)
def lead(rng, w, z, cd, q, g, a, b):
    w[q, g][:, a] = z[q, g][:, b]; cd[q, g][rng.integers(0, D, a.shape), a] = b
def coded(rng):
    h = rng.integers(0, 256, (N, 8, 8, V)); n = np.argsort(rng.random((N, 8, V)), axis=-1)
    h[:, :, 0] = n & 255; h[:, :, 1] = n >> 8
    return np.concatenate([h, 255 - h], axis=2)
def part(rng, z):
    return (z * rng.random(z.shape)).astype(np.int64)
def twice(rng, w, z, cd, q, g, o):
    a, b = ring(o, L); n = len(a); x = np.arange(n)[:, None]; j = np.arange(L)[None, :]
    c = np.argsort(rng.random((n, 16)), axis=1)[:, :L]
    lo = rng.integers(0, 2, (n, L)); st = np.where(rng.random((n, 1, 1)) < 0.5, 1, rng.integers(1, 127, (n, L, 2)))
    zz = rng.integers(0, 4, (n, 1, 16)) + np.zeros((n, L, 16), np.int64); ww = np.full((n, L, 16), 255)
    for k in range(L):
        zz[x, (j + k) % L, c] = (lo, lo + st[:, :, 0], lo + st[:, :, 0] + st[:, :, 1])[k] if k < 3 else lo
        if k: ww[x, (j + k) % L, c] = 0
    z[q, g][:, a] = zz.transpose(2, 0, 1); w[q, g][:, a] = ww.transpose(2, 0, 1)
    cd[q, g][:, a] = np.where(rng.random((D,) + a.shape) < 0.5, a, b); cd[q, g][rng.integers(0, D, a.shape), a] = b
def calm(rng, w, z, cd, g):
    sets = []
    for q in range(N):
        o = rng.permutation(V); n = int(rng.integers(2, CAP + 1))
        sets.append((n, np.concatenate([np.sort(o[:n]), np.sort(o[n:])])))
    for q in range(N):
        n, s = sets[q]; k = s[:CAP]; come = z[q - 1, g][:, sets[q - 1][1][:CAP]]
        w[q, g][:, k] = part(rng, np.minimum(z[q, g][:, k], come)); w[q, g][:, s[:n]] = come[:, :n]
        v = rng.permutation(s[CAP:])[:n]
        z[q, g][:, v] = come[:, :n]; w[q, g][:, v] = part(rng, come[:, :n])
        cd[q, g][rng.integers(0, D, n), s[:n]] = v
def plant(rng, w, z, cd):
    for q in range(N):
        share = rng.permutation(np.array([0.01, 0.05, 0.3, 0.9, 0.01, 0.1, 0.5, 0.9]))
        for g in range(8):
            o = rng.permutation(V); i = 0
            for m in range(2, L + 2):
                a, b = ring(o[i:i + m * K], m); i += m * K
                lead(rng, w, z, cd, q, g, a, b)
                w[q, g][:, a] = np.clip(w[q, g][:, a] + rng.integers(-3, 2, (16,) + a.shape), 0, 255)
            p = o[i:i + RO * K].reshape(RO, K); i += RO * K
            u = o[i:i + RO * K].reshape(RO, K); i += RO * K
            for j in range(RO):
                s = rng.permutation(D); v = u[max(j - 1, 0)]
                if j: z[q, g][:, u[j]] = np.maximum(z[q, g][:, v] - rng.integers(0, 4, (16, K)), 0)
                w[q, g][:, p[j]] = z[q, g][:, v]; w[q, g][:, u[j]] = z[q, g][:, p[j]]
                cd[q, g][s[0], p[j]] = v; cd[q, g][s[1], p[j]] = u[j]; cd[q, g][s[2], u[j]] = p[j]
            r = o[i:]; r = r[rng.random(len(r)) >= share[g]]
            w[q, g][:, r] = part(rng, z[q, g][:, r])
    return pack(w, z, cd)
def setup_inputs(rng):
    z = rng.integers(0, 256, (N, 8, 16, V)); w = rng.integers(0, 256, (N, 8, 16, V)); cd = rng.integers(0, V, (N, 8, D, V))
    return plant(rng, w, z, cd)
def setup_inputs_room(rng):
    z = coded(rng); w = part(rng, z); cd = rng.integers(0, V, (N, 8, D, V))
    for q in range(N):
        for g in range(8):
            n = int(rng.choice(np.array([0, 1, CAP - 1, CAP, CAP + 1, V // 2])))
            if q < 2: n = (CAP, CAP + 1, CAP - 1, 1, 0, V // 2, CAP, CAP + 1)[(g + q) % 8]
            o = rng.permutation(V); i = n
            if q < 2 and n:
                j = int(np.flatnonzero(o == V - 1)[0]); o[j] = o[0]; o[0] = V - 1
            lead(rng, w, z, cd, q, g, o[:n], rng.choice(o[n:], n))
            for m in range(2, L + 1):
                a, b = ring(o[i:i + m * K], m); i += m * K
                lead(rng, w, z, cd, q, g, a, b)
    return pack(w, z, cd)
def setup_inputs_rings(rng):
    z = coded(rng); w = part(rng, z); cd = rng.integers(0, V, (N, 8, D, V)); far = int(np.lcm.reduce(np.arange(1, L + 1)))
    calm(rng, w, z, cd, 5)
    for q in range(N):
        for g in range(8):
            if g == 5: continue
            if g == 4:
                w[q, g][:, :CAP] = 0
                twice(rng, w, z, cd, q, g, CAP + rng.permutation(V - CAP)); continue
            ms = [[L + 1], [2], [3], [L]][g] if g < 4 else [int(m) for m in rng.permutation(np.array(list(range(1, L + 3)) + [2 * L, 3 * L, far]))]
            o = rng.permutation(V); n = V // sum(ms); i = 0
            for m in ms:
                a, b = ring(o[i:i + n * m], m); i += n * m
                lead(rng, w, z, cd, q, g, a, b)
            if i < V:
                a, b = ring(o[i:], V - i); lead(rng, w, z, cd, q, g, a, b)
    return pack(w, z, cd)
def setup_inputs_ties(rng):
    z = np.zeros((N, 8, 16, V), np.int64); w = np.zeros((N, 8, 16, V), np.int64); cd = np.zeros((N, 8, D, V), np.int64); h = V // 2; t = V // 4
    for q in range(N):
        for g in range(8):
            o = rng.permutation(V); lo, hi = o[:h], o[h:]
            bl = np.concatenate([rng.integers(0, 61, 12), np.full(4, 255)]); bh = rng.integers(150, 255, 16)
            tl = np.stack([rng.permutation(bl) for _ in range(5)], axis=1); th = np.stack([rng.permutation(bh) for _ in range(5)], axis=1)
            zz, ww, cc = z[q, g], w[q, g], cd[q, g]
            zz[:, lo] = tl[:, rng.integers(0, 5, h)]; zz[:, hi] = th[:, rng.integers(0, 5, h)]
            cc[:, :] = rng.choice(lo, (D, V))
            a, b = lo[:t], hi[:t]; three = rng.random(t) < 0.5
            ww[:, a] = 255; ww[:, b] = zz[:, a]; cc[0, b] = a
            cc[D - 1, a] = np.where(rng.random(t) < 0.5, a, cc[D - 1, a])
            p = np.argsort(rng.random((t, D)), axis=1); x = np.sort(p[:, :3], axis=1); x2 = np.sort(p[:, :2], axis=1)
            x[~three] = x2[~three][:, [0, 1, 1]]
            which = np.where(three, rng.integers(0, 3, t), rng.integers(0, 2, t))
            v = np.where(np.arange(3)[:, None] == which[None, :], b[None, :], rng.choice(hi, (3, t))); v[2] = np.where(three, v[2], v[1])
            for i in range(3): cc[x[:, i], a] = v[i]
            e = hi[t:]; ww[:, e] = 255; cc[:, e] = np.roll(e.reshape(-1, 2), 1, axis=1).reshape(-1)[None, :]
            c = lo[t:]; ww[:, c] = np.concatenate([tl, th], axis=1)[:, rng.integers(0, 10, len(c))]
            cc[:, c] = rng.integers(0, V, (D, len(c))); cc[0, c] = np.where(rng.random(len(c)) < 0.3, c, cc[0, c]); cc[2, c] = np.where(rng.random(len(c)) < 0.5, cc[0, c], cc[2, c])
    return pack(w, z, cd)
def setup_inputs_ends(rng):
    z = rng.integers(0, 256, (N, 8, 16, V)); w = rng.integers(0, 256, (N, 8, 16, V)); cd = rng.integers(0, V, (N, 8, D, V))
    cd[:, ::2] = rng.choice(np.array([0, V - 1, V // 2, 3]), (N, 4, D, V))
    m = np.arange(V) ^ 1; m = np.where(rng.random(V) < 0.5, m, m[::-1])
    cd[:, 1::2, D - 1] = m; w[:, 1::2] = z[:, 1::2][:, :, :, m]
    w[:, 3::4] = part(rng, z[:, 3::4])
    w[:, 3::4, :, V - 1 - CAP // 2:V - 1] = z[:, 3::4, :, V // 2:V // 2 + 1]; cd[:, 3::4, 1, V - 1 - CAP // 2:V - 1] = V // 2
    w[..., 0] = z[..., V - 1]; w[..., V - 1] = z[..., 0]; cd[:, :, 0, 0] = V - 1; cd[:, :, 0, V - 1] = 0
    return pack(w, z, cd)
def setup_inputs_spread(rng):
    z = np.minimum((np.exp2(8 * rng.random((N, 8, 1, V))) * rng.random((N, 8, 16, V))).astype(np.int64), 255)
    w = np.minimum((np.exp2(8 * rng.random((N, 8, 1, V))) * rng.random((N, 8, 16, V))).astype(np.int64), 255)
    return plant(rng, w, z, rng.integers(0, V, (N, 8, D, V)))
def check_inputs(d):
    bad = []
    for k in ("wish", "goods"):
        v = d[k].astype(np.float32)
        if not np.all((v >= 0) & (v <= 255) & (v == np.floor(v))): bad.append("values of " + k)
    if np.min(d["cand"]) < 0 or np.max(d["cand"]) > V - 1: bad.append("range of cand")
    return bad
def reference(wish, goods, cand):
    w = wish.astype(np.float32).astype(np.int32).reshape(N, 8, 16, V); z = goods.astype(np.float32).astype(np.int32).reshape(N, 8, 16, V)
    cd = np.stack([gentries(a) for a in cand]).astype(np.int64).reshape(N, 8, D, V)
    own = np.zeros((N, 8, V), np.int64) + np.arange(V)
    for t in range(RO):
        best = np.add.reduce(np.maximum(w - z, 0), axis=2); f = own
        for d in range(D):
            c = cd[:, :, d]; s = np.add.reduce(np.maximum(w - np.take_along_axis(z, c[:, :, None, :], 3), 0), axis=2)
            f = np.where(s < best, c, f); best = np.minimum(s, best)
        h = f; back = np.zeros((N, 8, V), bool)
        for i in range(2, L + 1):
            h = np.take_along_axis(f, h, 2); back = back | (h == own)
        trade = (f != own) & back; unmet = (f != own) & ~back
        z = np.take_along_axis(z, np.where(trade, f, own)[:, :, None, :], 3)
        order = np.argsort(~unmet, axis=2, kind="stable")[:, :, None, :CAP]
        away = np.take_along_axis(z, order, 3)
        np.put_along_axis(z, np.broadcast_to(order, (N, 8, 16, CAP)), np.roll(away, 1 + t, axis=0), 3)
    return {"y": z.reshape(N, 128, V).astype(np.float32).astype(BF)}

@@ -1,0 +1,378 @@
+from concourse.mybir import AluOpType, ActivationFunctionType
+
+ALU = AluOpType
+ACT = ActivationFunctionType
+V, CAP, RO, N = 2048, 192, 2, 8
+NB = 140
+BF, F32, I32, U16 = "bfloat16", "float32", "int32", "uint16"
+NVJ = 5
+ZS = 80
+
+SCRATCH = {"q2": ("sbuf", [128, 8, 16, 16], BF), "pd": ("psum", [128, 2048], F32)}
+for _dt, _n, _names in (
+        (BF, V, "w z0 z1 z2 m0 m1 m2 m3 mo zg3 w0 xx yy zz"), (BF, V + CAP, "r0 r1"), (BF, 512, "cflag chi clo zg2"),
+        (BF, 128, "ones eye neye eye16 eye128 eye2k bo nsu a16 alo lob hib ut"), (BF, 16, "blk nblk cb e56"),
+        (BF, 256, "neye2"), (BF, 144, "e23 e1 c255 ub bb cuml"), (BF, 640, "cc"), (BF, CAP, "kw cmp inc"),
+        (BF, NB * NVJ, "rst fl fs"), (BF, NB * (12 - NVJ), "junk"),
+        (F32, 128, "bst dfa p4 p5 p6 tt ss"), (F32, 16, "rcol k16 kcol acc"),
+        (I32, 512, "candi"), (I32, 128, "besti loi hii"), (I32, 16, "pint rint vi oi"),
+        (U16, 512, "candu"), (U16, 128, "su0 su1 sf f2u"), (U16, 16, "ls0 ls1 lv0 lv1 vu0 vu1 cu ou")):
+    for _name in _names.split():
+        SCRATCH[_name] = ("sbuf", [128, _n], _dt)
+for _name in ("pa", "pb", "pc", "pe"):
+    SCRATCH[_name] = ("psum", [128, 512], F32)
+SEMAPHORES = ["sV", "sS", "sT", "sG", "ldc", "ldz", "ldwa", "ldwb", "sent", "stored",
+              "az0", "az1", "as0", "as1", "av0", "av1"]
+
+
+def rank_program(g, core, T, topo):
+    rank = T.rank_of(core)
+    if rank is None:
+        return
+    queue = {"V": g.vector, "S": g.scalar, "T": g.tensor, "G": g, "Y": g.sync}
+    count = {"V": 0, "S": 0, "T": 0, "G": 0}
+    seen = {e: {} for e in queue}
+    writer, readers, bank = {}, {}, {}
+
+    def wait(e, tok):
+        if seen[e].get(tok[0], 0) < tok[1]:
+            queue[e].wait_ge(T.sem[tok[0]], tok[1])
+            seen[e][tok[0]] = tok[1]
+
+    def need(e, rd, wr=(), ps=()):
+        toks = [writer[k] for k in rd]
+        for k in wr:
+            toks += readers.get(k, []) + ([writer[k]] if k in writer else [])
+        for k in ps:
+            toks += [t for o, t in bank.get(k, {}).items() if o != e]
+        best = {}
+        for s, n, o in toks:
+            if not (e == "T" and o == "T"):
+                best[s] = max(best.get(s, 0), n)
+        for s, n in best.items():
+            wait(e, (s, n))
+
+    def op(e, fn, rd=(), wr=(), ps=()):
+        need(e, rd, wr, ps)
+        fn().then_inc(T.sem["s" + e], 1)
+        count[e] += 1
+        tok = ("s" + e, count[e], e)
+        for k in rd:
+            readers.setdefault(k, []).append(tok)
+        for k in wr:
+            writer[k] = tok
+            readers[k] = []
+        for k in ps:
+            bank.setdefault(k, {})[e] = tok
+
+    def mm(items, rd, ps):
+        def run():
+            last = None
+            for o, l, r, a, b in items:
+                last = g.tensor.matmul(o, l, r, a, b)
+            return last
+        op("T", run, rd, (), ps)
+
+    vec, act = g.vector, g.scalar
+
+    def ts(o, i, s1, s2, o0, o1, rd, wr, ps=()):
+        if s2 is None:
+            op("V", lambda: vec.tensor_scalar(o, i, s1, None, o0), rd, wr, ps)
+        else:
+            op("V", lambda: vec.tensor_scalar(o, i, s1, s2, o0, o1), rd, wr, ps)
+
+    def tt(o, a, b, alu, rd, wr, ps=()):
+        op("V", lambda: vec.tensor_tensor(o, a, b, alu), rd, wr, ps)
+
+    def cp(o, i, rd, wr, ps=()):
+        op("V", lambda: vec.tensor_copy(o, i), rd, wr, ps)
+
+    def scp(o, i, rd, wr, ps=(), fn=ACT.Copy):
+        op("S", lambda: act.activation(o, i, fn), rd, wr, ps)
+
+    def iota(o, pat, base, ch, wr, small=True):
+        if small:
+            op("G", lambda: g.iota(o, pat, base, ch, allow_small_or_imprecise_dtypes=True), (), wr)
+        else:
+            op("G", lambda: g.iota(o, pat, base, ch), (), wr)
+
+    def sel(o, i, pat, alu, fill, base, ch, rd, wr):
+        op("G", lambda: g.affine_select(o, i, pat, alu, fill, base, ch), rd, wr)
+
+    nsent = [0]
+
+    def send(dst, o, i, sem, rd):
+        d = T.cores[dst]
+        rid, pid = topo.addr(d, core)
+        need("G", rd)
+        g.remote_dma(o, i, T.sem[sem], T.sem.sent, pid, rid, topo.mask(core, d))
+        nsent[0] += len(topo.engines(core, d))
+
+    g.sync.dma_start(T.candi[:], T.cand[:]).then_inc(T.sem.ldc, 16)
+    g.scalar.dma_start(T.z0[:], T.goods[:]).then_inc(T.sem.ldz, 16)
+    g.sync.dma_start(T.w[:, 0:1024], T.wish[:, 0:1024]).then_inc(T.sem.ldwa, 16)
+    g.sync.dma_start(T.w[:, 1024:V], T.wish[:, 1024:V]).then_inc(T.sem.ldwb, 16)
+    writer["candi"], writer["z0"] = ("ldc", 16, ""), ("ldz", 16, "")
+    writer["wa"], writer["wb"] = ("ldwa", 16, ""), ("ldwb", 16, "")
+    for t in range(RO):
+        n = len(topo.engines(T.cores[(rank - 1 - t) % N], core))
+        writer["r%d" % t], writer["ls%d" % t], writer["lv%d" % t] = ("az%d" % t, n, ""), ("as%d" % t, n, ""), ("av%d" % t, n, "")
+
+    def wk(a0, a1):
+        return (["wa"] if a0 < 1024 else []) + (["wb"] if a1 > 1024 else [])
+
+    op("V", lambda: vec.memset(T.ones[:], 1.0), (), ["ones"])
+    iota(T.pint[:, 0:1], [[0, 1]], 0, 1, ["pint"], small=False)
+    iota(T.a16[:], [[16, 128]], 0, 0, ["a16"])
+    sel(T.eye[:], T.ones[:], [[-1, 128]], ALU.is_equal, 0.0, 0, 1, ["ones"], ["eye"])
+    sel(T.bo[:], T.ones[:], [[-16, 8], [0, 16]], ALU.is_ge, 0.0, 0, 1, ["ones"], ["bo"])
+    sel(T.bo[:], T.bo[:], [[16, 8], [0, 16]], ALU.is_ge, 0.0, 15, -1, ["bo"], ["bo"])
+    op("V", lambda: vec.memset(T.cc[0:64, :], -262144.0), (), ["cc0"])
+    for j, p in enumerate((4, 0, 3, 2, 1)):
+        op("V", lambda j=j, p=p: vec.memset(T.cc[64:128, 128 * j:128 * j + 128], 32.0 * p), (), ["cc%d" % (j + 1)])
+    ccs = ["cc%d" % j for j in range(6)]
+    ts(T.rint[:, 0:1], T.pint[:, 0:1], 15, None, ALU.bitwise_and, None, ["pint"], ["rint"])
+    cp(T.rcol[:, 0:1], T.rint[:, 0:1], ["rint"], ["rcol"])
+    ts(T.rcol[:, 1:2], T.rint[:, 0:1], 0.5, None, ALU.add, None, ["rint"], ["rhalf"])
+    op("S", lambda: act.activation(T.alo[:], T.ones[:], ACT.Identity, scale=T.rcol[:, 0:1]), ["ones", "rcol"], ["alo"])
+    for nm, s in (("neye", -1.0), ("eye2k", 2048.0)):
+        op("S", lambda nm=nm, s=s: act.activation(T[nm][:], T.eye[:], ACT.Copy, scale=s), ["eye"], [nm])
+    for nm, c, s in (("blk", 0, 8192.0), ("blk", 8, 8192.0), ("nblk", 0, -8192.0)):
+        op("S", lambda nm=nm, c=c, s=s: act.activation(T[nm][:, c:c + 8], T.bo[:, 0::16], ACT.Copy, scale=s), ["bo"], [nm])
+    for nm, s in (("eye16", 16.0), ("eye128", 128.0)):
+        op("S", lambda nm=nm, s=s: act.activation(T[nm][:], T.eye[:], ACT.Copy, scale=s), ["eye"], [nm])
+    mm([(T.pe[:, 0:128], T.eye[:], T.a16[:], True, False), (T.pe[:, 0:128], T.eye[:], T.alo[:], False, True)],
+       ["eye", "a16", "alo"], ["PE"])
+    cp(T.candu[:], T.candi[:], ["candi"], ["candu"])
+    cp(T.chi[:], T.candi[:], ["candi"], ["chi"])
+    mm([(T.pc[:], T.eye[:], T.chi[:], True, True)], ["chi"], ["PC"])
+    for d in range(4):
+        tt(T.cflag[:, 128 * d:128 * d + 128], T.candi[:, 128 * d:128 * d + 128], T.pe[:, 0:128], ALU.is_le,
+           ["candi"], ["cflag%d" % d], ["PE"])
+    tt(T.clo[:], T.candi[:], T.pc[:], ALU.subtract, ["candi"], ["clo"], ["PC"])
+
+    def later_constants():
+        iota(T.q2[:], [[0, 2048]], 0, 0, ["q2"])
+        iota(T.q2[:, :, 0, :], [[0, 8], [1, 16]], 0, 0, ["q2"])
+        iota(T.q2[:, :, 1, :], [[0, 128]], 0, 1, ["q2"])
+        iota(T.e23[:], [[0, 144]], 0, 0, ["e23"])
+        iota(T.e56[:], [[0, 16]], 0, 0, ["e56"])
+        for nm, col, p in (("e23", T.e23[:, 15:143:16], 2), ("e56", T.e56[:, 0:8], 0), ("e56", T.e56[:, 8:16], 2)):
+            sel(col, col, [[-16, 8]], ALU.not_equal, 1.0, -p, 1, [nm], [nm])
+            sel(col, col, [[-16, 8]], ALU.not_equal, 16.0, -p - 1, 1, [nm], [nm])
+        iota(T.neye2[:], [[0, 256]], -1, 0, ["neye2"])
+        sel(T.neye2[:], T.neye2[:], [[0, 2], [-1, 128]], ALU.is_equal, 0.0, 0, 1, ["neye2"], ["neye2"])
+        iota(T.e1[:], [[0, 144]], 0, 0, ["e1"])
+        sel(T.e1[:, 15:143:16], T.bo[:, 0::16], [[0, 8]], ALU.is_ge, 0.0, 0, 0, ["bo"], ["e1"])
+        iota(T.nsu[:], [[0, 128]], -1, 0, ["nsu"])
+        sel(T.nsu[:], T.nsu[:], [[-1, 128]], ALU.is_gt, 0.0, 0, 1, ["nsu"], ["nsu"])
+        sel(T.nsu[:], T.nsu[:], [[16, 8], [0, 16]], ALU.is_ge, 0.0, 15, -1, ["nsu"], ["nsu"])
+        iota(T.kw[:], [[1, CAP]], 0, 0, ["kw"])
+        iota(T.c255[:], [[0, 144]], 255, 0, ["c255"])
+        iota(T.rst[:], [[0, NB * NVJ]], 1, 0, ["rst"])
+        iota(T.rst[:, 0::NB], [[0, NVJ]], 0, 0, ["rst"])
+        iota(T.k16[:], [[16, 16]], 0, 0, ["k16"])
+
+    plane = {"o": ("PA", T.pa, 0), 3: ("PA", T.pa, 128), 0: ("PB", T.pb, 0), 1: ("PB", T.pb, 128), 2: ("PC", T.pc, 0)}
+
+    def low(d):
+        b, buf, c0 = plane[d]
+        o = buf[:, c0:c0 + 128]
+        if d == "o":
+            return [(o, T.a16[:], T.eye[:], False, False), (o, T.alo[:], T.eye[:], False, False)]
+        s = slice(128 * d, 128 * d + 128)
+        return [(o, T.cflag[:, s], T.eye2k[:], False, False), (o, T.chi[:, s], T.eye[:], False, False),
+                (o, T.clo[:, s], T.eye[:], False, False)]
+
+    lowrd = ["ones", "a16", "alo", "eye", "eye2k", "chi", "clo"] + ccs + ["cflag%d" % d for d in range(4)]
+
+    def preload():
+        mm([(T.pa[:, 0:256], T.ones[:], T.cc[:, 0:256], True, False)] + low("o") + low(3), lowrd, ["PA"])
+        mm([(T.pc[:, 0:128], T.ones[:], T.cc[:, 512:640], True, False)] + low(2), lowrd, ["PC"])
+        mm([(T.pb[:, 0:256], T.ones[:], T.cc[:, 256:512], True, False)] + low(0) + low(1), lowrd, ["PB"])
+
+    def sums(d, src, w8, c0, c1, rd, stop=False):
+        b, buf, o0 = plane[d]
+        mm([(buf[c0:c1, o0 + r:o0 + 128:16], src[:, 16 * c0 + r:16 * c1:16], T[w8][:, 0:8], False, stop and r == 15)
+            for r in range(16)], rd + [w8], [b])
+
+    def diffs(src, s0, w0, n, b0, rd):
+        it = []
+        for j in range(n):
+            o = T.pd[:, 512 * (b0 + j):512 * (b0 + j + 1)]
+            it += [(o, T.eye[:], T.w[:, w0 + 512 * j:w0 + 512 * (j + 1)], True, False),
+                   (o, T.neye[:], src[:, s0 + 512 * j:s0 + 512 * (j + 1)], False, True)]
+        mm(it, rd + wk(w0, w0 + 512 * n) + ["eye", "neye"], ["D%d" % (b0 + j) for j in range(n)])
+
+    def relu(dst, c0, n, b0, key):
+        scp(dst[:, c0:c0 + 512 * n], T.pd[:, 512 * b0:512 * (b0 + n)], [], [key], ["D%d" % (b0 + j) for j in range(n)], ACT.Relu)
+
+    def tolist(out, src, e, c0, c1, first, last):
+        return [(out[:, c0:c1], T[e][:, 15 - r:143 - r], src[:, 16 * c0 + r:16 * c1:16], first and r == 0, last and r == 15)
+                for r in range(16)]
+
+    def gather(e, dst, win, off, c0, c1, rd, key, d0=0):
+        o, i = dst[:, d0 + 16 * c0:d0 + 16 * c1], win.indirect(off[:, c0:c1])
+        if e == "V":
+            cp(o, i, rd, [key])
+        else:
+            scp(o, i, rd, [key])
+
+    ww = ["wa", "wb"]
+
+    def wish_sums():
+        mm([(T.pa[:, r:256:16], T.w[:, r::16], T.blk[:], False, False) for r in range(16)], ww + ["blk"], ["PA"])
+        sums(2, T.w, "blk", 96, 128, ww)
+
+    zbuf = [T.z0, T.z1, T.z2]
+    for t in range(RO):
+        z, zn, zk, znk = zbuf[t], zbuf[t + 1], "z%d" % t, "z%d" % (t + 1)
+        to = (rank + 1 + t) % N
+        rwin, su, vu, ls, lv = T["r%d" % t], T["su%d" % t], T["vu%d" % t], T["ls%d" % t], T["lv%d" % t]
+        zw = z[:, 0:V]
+        send(to, rwin[:, 0:V], z[:, 0:V], "az%d" % t, [zk] + ww)
+        if t == 0:
+            later_constants()
+
+        def gmin(d, c0, c1, key):
+            tt(T["m%d" % d][:, 16 * c0:16 * c1], zw.indirect(T.candu[:, 128 * d + c0:128 * d + c1]), T.w[:, 16 * c0:16 * c1],
+               ALU.min, [zk, "candu"] + wk(16 * c0, 16 * c1), [key])
+
+        def gsc(dst, d, c0, c1, o0, key):
+            scp(dst[:, o0:o0 + 16 * (c1 - c0)], zw.indirect(T.candu[:, 128 * d + c0:128 * d + c1]), [zk, "candu"], [key])
+
+        if t == 0:
+            gmin(0, 0, 64, "m0a")
+            gmin(0, 64, 128, "m0")
+        else:
+            need("V", [], ["m0a"])
+            gmin(0, 0, 128, "m0")
+        gsc(T.zg3, 3, 0, 128, 0, "g3")
+        if t == 0:
+            preload()
+        diffs(z, 0, 0, 2, 0, [zk])
+        diffs(z, 1024, 1024, 2, 2, [zk])
+        relu(T.mo, 0, 2, 0, "moa")
+        sums(0, T.m0, "blk", 0, 128, ["m0a", "m0"])
+        diffs(T.zg3, 0, 0, 2, 0, ["g3"])
+        relu(T.mo, 1024, 2, 2, "mob")
+        gsc(T.zg2, 2, 96, 128, 0, "g2")
+        diffs(T.zg3, 1024, 1024, 2, 2, ["g3"])
+        relu(T.m3, 0, 2, 0, "m3a")
+        gmin(1, 0, 128, "m1")
+        gmin(2, 0, 64, "m2a")
+        if t == 0:
+            wish_sums()
+        sums(1, T.m1, "blk", 0, 128, ["m1"], stop=True)
+        sums("o", T.mo, "nblk", 0, 128, ["moa", "mob"])
+        diffs(T.zg2, 0, 1536, 1, 0, ["g2"])
+        cp(T.bst[:], T.pb[:, 0:128], [], ["bst"], ["PB"])
+        tt(T.bst[:], T.pb[:, 128:256], T.bst[:], ALU.max, ["bst"], ["bst"], ["PB"])
+        gmin(2, 64, 96, "m2b")
+        relu(T.m3, 1024, 2, 2, "m3b")
+        relu(T.m2, 1536, 1, 0, "m2c")
+        sums(2, T.m2, "blk", 0, 64, ["m2a"], stop=True)
+        sums(3, T.m3, "nblk", 0, 128, ["m3a", "m3b"], stop=True)
+        sums(2, T.m2, "nblk", 96, 128, ["m2c"], stop=True)
+        sums(2, T.m2, "blk", 64, 96, ["m2b"], stop=True)
+        tt(T.bst[:], T.pa[:, 0:128], T.bst[:], ALU.max, ["bst"], ["bst"], ["PA"])
+        tt(T.bst[:], T.pa[:, 128:256], T.bst[:], ALU.max, ["bst"], ["bst"], ["PA"])
+        tt(T.besti[:], T.pc[:, 0:128], T.bst[:], ALU.max, ["bst"], ["besti"], ["PC"])
+        ts(T.loi[:], T.besti[:], 15, None, ALU.bitwise_and, None, ["besti"], ["loi"])
+        ts(T.hii[:], T.besti[:], 4, 127, ALU.arith_shift_right, ALU.bitwise_and, ["besti"], ["hii"])
+        need("V", ["q2"])
+        cp(T.q2[:, :, 2, :], T.loi[:], ["loi"], ["qlo"])
+        cp(T.q2[:, :, 3, :], T.hii[:], ["hii"], ["qhi"])
+        q = ["q2", "qlo", "qhi"]
+        cp(T.lob[:], T.q2[:, :, 2, :], ["qlo"], ["lob"])
+        cp(T.hib[:], T.q2[:, :, 3, :], ["qhi"], ["hib"])
+        for b in range(4):
+            mm([(T.pd[:, 128 * r:128 * r + 128], T.q2[:, :, :, r], T.eye[:], True, True) for r in range(4 * b, 4 * b + 4)],
+               q, ["D%d" % b])
+            if b == 0:
+                mm([(T.pe[:, 0:128], T.lob[:], T.eye128[:], True, False),
+                    (T.pe[:, 0:128], T.hib[:], T.eye[:], False, True)], ["lob", "hib", "eye128"], ["PE"])
+        mm([(T.pb[:, 128:256], T.lob[:], T.eye[:], True, False),
+            (T.pb[:, 128:256], T.hib[:], T.eye16[:], False, True),
+            (T.pb[:, 0:128], T.lob[:], T.eye[:], True, False),
+            (T.pb[:, 0:128], T.hib[:], T.eye16[:], False, False),
+            (T.pb[:, 0:128], T.neye[:], T.a16[:], False, False),
+            (T.pb[:, 0:128], T.neye[:], T.alo[:], False, True)], ["lob", "hib", "eye16"], ["PB"])
+        cp(T.sf[:], T.pe[:, 0:128], [], ["sf"], ["PE"])
+        for b in range(4):
+            (scp if b % 2 == 0 else cp)(T.w0[:, 512 * b:512 * b + 512], T.pd[:, 512 * b:512 * b + 512], [], ["w0%d" % b], ["D%d" % b])
+        turned = [T.pd[:, 0:128], T.pd[:, 512:640], T.pd[:, 1024:1152], T.pd[:, 1152:1280]]
+        mm([(turned[0], T.eye[:], T.lob[:], True, False), (turned[0], T.eye16[:], T.hib[:], False, False),
+            (turned[0], T.a16[:], T.neye[:], False, False), (turned[0], T.alo[:], T.neye[:], False, True)], [], ["D0"])
+        mm([(turned[1], T.a16[:], T.neye[:], True, False), (turned[1], T.alo[:], T.neye[:], False, False)], [], ["D1"])
+        mm([(T.pd[:, 1024:1280], T.a16[:], T.neye2[:], True, False), (T.pd[:, 1024:1280], T.alo[:], T.neye2[:], False, False)],
+           ["neye2"], ["D2"])
+        w0k = ["w0%d" % b for b in range(4)] + ["sf"]
+        for h in range(2):
+            gather("V", T.xx, T.w0[:, 0:V], T.sf, 64 * h, 64 * h + 32, w0k, "x%d" % (2 * h))
+            gather("S", T.xx, T.w0[:, 0:V], T.sf, 64 * h + 32, 64 * h + 64, w0k, "x%d" % (2 * h + 1))
+            mm(tolist(T.pe, T.xx, "e23", 64 * h, 64 * h + 64, True, True), ["x%d" % (2 * h), "x%d" % (2 * h + 1), "e23"], ["PE"])
+        scp(T.dfa[:], turned[0], [], ["dfa"], ["D0"])
+        cp(T.f2u[:], T.pe[:, 0:128], [], ["f2u"], ["PE"])
+        xk = ["x0", "x1", "x2", "x3", "f2u"]
+        if t == 0:
+            op("S", lambda: act.activation(T.kcol[:], T.k16[:], ACT.Identity, bias=T.rcol[:, 1:2]), ["k16", "rhalf"], ["kcol"])
+        gather("V", T.yy, T.xx[:, 0:V], T.f2u, 0, 64, xk, "y0")
+        gather("S", T.yy, T.xx[:, 0:V], T.f2u, 64, 128, xk, "y1")
+        yk = ["y0", "y1", "f2u"]
+        mm([(T.pd[:, 512 + r:640:16], T.yy[:, r::16], T.e56[:, 8:16], False, r == 15) for r in range(16)], ["y0", "y1", "e56"], ["D1"])
+        gather("V", T.zz, T.yy[:, 0:V], T.f2u, 0, 64, yk, "c0")
+        gather("S", T.zz, T.yy[:, 0:V], T.f2u, 64, 128, yk, "c1")
+        mm([(T.pd[:, 1024 + r:1280:16], T.zz[:, r::16], T.e56[:], False, r == 15) for r in range(16)], ["c0", "c1"], ["D2"])
+        tt(T.p4[:], turned[1], T.dfa[:], ALU.mult, ["dfa"], ["p4"], ["D1"])
+        tt(T.p5[:], turned[2], T.p4[:], ALU.mult, ["p4"], ["p5"], ["D2"])
+        tt(T.p6[:], turned[3], T.p5[:], ALU.mult, ["p5"], ["p6"], ["D2"])
+        ts(T.ut[:], T.p6[:], 0.0, None, ALU.not_equal, None, ["p6"], ["ut"])
+        mm([(T.pe[:, 0:128], T.ut[:], T.eye[:], True, True)], ["ut"], ["PE"])
+        cp(T.ub[:, 0:128], T.pe[:, 0:128], [], ["ub"], ["PE"])
+        ts(T.ub[:, 128:NB], T.pe[:, 0:NB - 128], 0.0, None, ALU.is_equal, None, [], ["ue"], ["PE"])
+        mm([(T.pd[:, 1536:1536 + NB], T.bo[:], T.ub[:, 0:NB], True, True),
+            (T.pd[:, 1792:1792 + NB], T.nsu[:], T.ub[:, 0:NB], True, True)], ["ub", "ue", "bo", "nsu"], ["D3"])
+        tt(T.tt[:], T.pb[:, 0:128], T.ub[:, 0:128], ALU.mult, ["ub"], ["tt"], ["PB"])
+        op("V", lambda: vec.tensor_tensor_scan(T.bb[:, 0:NB], T.pd[:, 1536:1536 + NB], T.c255[:, 0:NB], 0.0, ALU.add, ALU.min),
+           ["c255"], ["bb"], ["D3"])
+        for j in range(NVJ, 12):
+            op("S", lambda j=j: act.activation(T.junk[:, NB * (j - NVJ):NB * (j - NVJ + 1)], T.bb[:, 0:NB], ACT.Sign,
+                                               bias=T.kcol[:, j:j + 1], scale=-1.0, accum_out=T.acc[:, j:j + 1]),
+               ["bb", "kcol"], ["acc%d" % j])
+        for j in range(NVJ):
+            ts(T.fl[:, NB * j:NB * (j + 1)], T.bb[:, 0:NB], T.kcol[:, j:j + 1], None, ALU.is_le, None, ["bb", "kcol"], ["fl%d" % j])
+        op("V", lambda: vec.tensor_tensor_scan(T.fs[:], T.rst[:], T.fl[:], 0.0, ALU.mult, ALU.add),
+           ["rst"] + ["fl%d" % j for j in range(NVJ)], ["fs"])
+        tt(T.cuml[:, 0:NB], T.pd[:, 1792:1792 + NB], T.bb[:, 0:NB], ALU.add, ["bb"], ["cuml"], ["D3"])
+        acck = ["acc%d" % j for j in range(NVJ, 12)]
+        cp(T.cu[:, 0:NVJ], T.fs[:, NB - 1::NB], ["fs"], ["cua"])
+        ts(T.cu[:, NVJ:12], T.acc[:, NVJ:12], 0.5, NB / 2.0, ALU.mult, ALU.add, acck, ["cub"])
+        scp(T.cb[:, 0:NVJ], T.fs[:, NB - 1::NB], ["fs"], ["cba"])
+        op("S", lambda: act.activation(T.cb[:, NVJ:12], T.acc[:, NVJ:12], ACT.Copy, bias=NB / 2.0, scale=0.5), acck, ["cbb"])
+        tt(T.cmp[:], T.cuml[:, 0:NB].indirect(T.cu[:, 0:12]), T.kw[:], ALU.is_le, ["cuml", "cua", "cub", "kw"], ["cmp"])
+        mm([(T.pe[:, 0:12], T.eye16[:], T.cb[:, 0:12], True, False)] + tolist(T.pe, T.cmp, "e1", 0, 12, False, True),
+           ["cba", "cbb", "cmp", "e1"], ["PE"])
+        tt(T.ss[:], T.pb[:, 128:256], T.tt[:], ALU.subtract, ["tt"], ["ss"], ["PB"])
+        cp(su[:], T.ss[:], ["ss"], ["su%d" % t])
+        send(to, ls[:, 0:12], su[:, 0:12], "as%d" % t, ["su%d" % t])
+        cp(vu[:, 0:12], T.pe[:, 0:12], [], ["vu%d" % t], ["PE"])
+        send(to, lv[:, 0:12], vu[:, 0:12], "av%d" % t, ["vu%d" % t])
+        gather("S", zn, zw, su, 0, ZS, [zk, "su%d" % t], znk + "a")
+        cp(T.vi[:, 0:12], T.pe[:, 0:12], [], ["vi"], ["PE"])
+        ts(T.oi[:, 0:12], T.vi[:, 0:12], V - 1, None, ALU.bitwise_and, None, ["vi"], ["oi"])
+        cp(T.ou[:, 0:12], T.oi[:, 0:12], ["oi"], ["ou"])
+        gather("V", zn, zw, su, ZS, 128, [zk, "su%d" % t], znk + "b")
+        if t + 1 < RO:
+            preload()
+            wish_sums()
+        gather("V", rwin, rwin[:, 0:V], ls, 0, 12, ["r%d" % t, "ls%d" % t], "rx%d" % t, d0=V)
+        gather("V", T.inc, rwin[:, 0:V + CAP], lv, 0, 12, ["r%d" % t, "rx%d" % t, "lv%d" % t], "inc")
+        cp(zn[:, 0:V].indirect(T.ou[:, 0:12]), T.inc[:], ["inc", "ou", znk + "a", znk + "b"], [znk])
+
+    need("Y", ["z%d" % RO])
+    g.sync.dma_start(T.y[:], zbuf[RO][:]).then_inc(T.sem.stored, 16)
+    for e in ("V", "S", "T", "G"):
+        wait("G", ("s" + e, count[e]))
+    g.wait_ge(T.sem.sent, nsent[0])
+    g.wait_ge(T.sem.stored, 16)

@@ -6,7 +6,7 @@ V, CAP, RO, N = 2048, 192, 2, 8
 NB = 140
 BF, F32, I32, U16 = "bfloat16", "float32", "int32", "uint16"
 NVJ = 5
-ZS = 80
+ZS = 108
 
 SCRATCH = {"q2": ("sbuf", [128, 8, 16, 16], BF), "pd": ("psum", [128, 2048], F32)}
 for _dt, _n, _names in (
@@ -14,7 +14,7 @@ for _dt, _n, _names in (
         (BF, 128, "ones eye neye eye16 eye128 eye2k bo nsu a16 alo lob hib ut"), (BF, 16, "blk nblk cb e56"),
         (BF, 256, "neye2"), (BF, 144, "e23 e1 c255 ub bb cuml"), (BF, 640, "cc"), (BF, CAP, "kw cmp inc"),
         (BF, NB * NVJ, "rst fl fs"), (BF, NB * (12 - NVJ), "junk"),
-        (F32, 128, "bst dfa p4 p5 p6 tt ss"), (F32, 16, "rcol k16 kcol acc"),
+        (F32, 128, "bst dfa p4 p5 tt ss"), (F32, 16, "rcol k16 kcol acc"),
         (I32, 512, "candi"), (I32, 128, "besti loi hii"), (I32, 16, "pint rint vi oi"),
         (U16, 512, "candu"), (U16, 128, "su0 su1 sf f2u"), (U16, 16, "ls0 ls1 lv0 lv1 vu0 vu1 cu ou")):
     for _name in _names.split():
@@ -141,14 +141,13 @@ def rank_program(g, core, T, topo):
         op("S", lambda nm=nm, c=c, s=s: act.activation(T[nm][:, c:c + 8], T.bo[:, 0::16], ACT.Copy, scale=s), ["bo"], [nm])
     for nm, s in (("eye16", 16.0), ("eye128", 128.0)):
         op("S", lambda nm=nm, s=s: act.activation(T[nm][:], T.eye[:], ACT.Copy, scale=s), ["eye"], [nm])
-    mm([(T.pe[:, 0:128], T.eye[:], T.a16[:], True, False), (T.pe[:, 0:128], T.eye[:], T.alo[:], False, True)],
+    mm([x for d in range(4) for x in ((T.pe[:, 128 * d:128 * d + 128], T.eye[:], T.a16[:], True, False),
+                                      (T.pe[:, 128 * d:128 * d + 128], T.eye[:], T.alo[:], False, True))],
        ["eye", "a16", "alo"], ["PE"])
     cp(T.candu[:], T.candi[:], ["candi"], ["candu"])
     cp(T.chi[:], T.candi[:], ["candi"], ["chi"])
     mm([(T.pc[:], T.eye[:], T.chi[:], True, True)], ["chi"], ["PC"])
-    for d in range(4):
-        tt(T.cflag[:, 128 * d:128 * d + 128], T.candi[:, 128 * d:128 * d + 128], T.pe[:, 0:128], ALU.is_le,
-           ["candi"], ["cflag%d" % d], ["PE"])
+    tt(T.cflag[:], T.candi[:], T.pe[:], ALU.is_le, ["candi"], ["cflag"], ["PE"])
     tt(T.clo[:], T.candi[:], T.pc[:], ALU.subtract, ["candi"], ["clo"], ["PC"])
 
     def later_constants():
@@ -184,7 +183,7 @@ def rank_program(g, core, T, topo):
         return [(o, T.cflag[:, s], T.eye2k[:], False, False), (o, T.chi[:, s], T.eye[:], False, False),
                 (o, T.clo[:, s], T.eye[:], False, False)]
 
-    lowrd = ["ones", "a16", "alo", "eye", "eye2k", "chi", "clo"] + ccs + ["cflag%d" % d for d in range(4)]
+    lowrd = ["ones", "a16", "alo", "eye", "eye2k", "chi", "clo", "cflag"] + ccs
 
     def preload():
         mm([(T.pa[:, 0:256], T.ones[:], T.cc[:, 0:256], True, False)] + low("o") + low(3), lowrd, ["PA"])
@@ -266,10 +265,10 @@ def rank_program(g, core, T, topo):
         sums(1, T.m1, "blk", 0, 128, ["m1"], stop=True)
         sums("o", T.mo, "nblk", 0, 128, ["moa", "mob"])
         diffs(T.zg2, 0, 1536, 1, 0, ["g2"])
-        cp(T.bst[:], T.pb[:, 0:128], [], ["bst"], ["PB"])
-        tt(T.bst[:], T.pb[:, 128:256], T.bst[:], ALU.max, ["bst"], ["bst"], ["PB"])
-        gmin(2, 64, 96, "m2b")
         relu(T.m3, 1024, 2, 2, "m3b")
+        scp(T.bst[:], T.pb[:, 0:128], [], ["bst"], ["PB"])
+        gmin(2, 64, 96, "m2b")
+        tt(T.bst[:], T.pb[:, 128:256], T.bst[:], ALU.max, ["bst"], ["bst"], ["PB"])
         relu(T.m2, 1536, 1, 0, "m2c")
         sums(2, T.m2, "blk", 0, 64, ["m2a"], stop=True)
         sums(3, T.m3, "nblk", 0, 128, ["m3a", "m3b"], stop=True)
@@ -292,54 +291,59 @@ def rank_program(g, core, T, topo):
             if b == 0:
                 mm([(T.pe[:, 0:128], T.lob[:], T.eye128[:], True, False),
                     (T.pe[:, 0:128], T.hib[:], T.eye[:], False, True)], ["lob", "hib", "eye128"], ["PE"])
+        turned = [T.pc[:, 0:128], T.pd[:, 512:640], T.pd[:, 1024:1152], T.pd[:, 1152:1280]]
+        mm([(turned[0], T.eye[:], T.lob[:], True, False), (turned[0], T.eye16[:], T.hib[:], False, False),
+            (turned[0], T.a16[:], T.neye[:], False, False), (turned[0], T.alo[:], T.neye[:], False, True)], ["eye16"], ["PC"])
         mm([(T.pb[:, 128:256], T.lob[:], T.eye[:], True, False),
             (T.pb[:, 128:256], T.hib[:], T.eye16[:], False, True),
             (T.pb[:, 0:128], T.lob[:], T.eye[:], True, False),
             (T.pb[:, 0:128], T.hib[:], T.eye16[:], False, False),
             (T.pb[:, 0:128], T.neye[:], T.a16[:], False, False),
-            (T.pb[:, 0:128], T.neye[:], T.alo[:], False, True)], ["lob", "hib", "eye16"], ["PB"])
+            (T.pb[:, 0:128], T.neye[:], T.alo[:], False, True)], ["lob", "hib"], ["PB"])
         cp(T.sf[:], T.pe[:, 0:128], [], ["sf"], ["PE"])
         for b in range(4):
             (scp if b % 2 == 0 else cp)(T.w0[:, 512 * b:512 * b + 512], T.pd[:, 512 * b:512 * b + 512], [], ["w0%d" % b], ["D%d" % b])
-        turned = [T.pd[:, 0:128], T.pd[:, 512:640], T.pd[:, 1024:1152], T.pd[:, 1152:1280]]
-        mm([(turned[0], T.eye[:], T.lob[:], True, False), (turned[0], T.eye16[:], T.hib[:], False, False),
-            (turned[0], T.a16[:], T.neye[:], False, False), (turned[0], T.alo[:], T.neye[:], False, True)], [], ["D0"])
+        scp(T.dfa[:], turned[0], [], ["dfa"], ["PC"])
         mm([(turned[1], T.a16[:], T.neye[:], True, False), (turned[1], T.alo[:], T.neye[:], False, False)], [], ["D1"])
         mm([(T.pd[:, 1024:1280], T.a16[:], T.neye2[:], True, False), (T.pd[:, 1024:1280], T.alo[:], T.neye2[:], False, False)],
            ["neye2"], ["D2"])
         w0k = ["w0%d" % b for b in range(4)] + ["sf"]
+        f2p = [("PE", T.pe), ("PA", T.pa)]
         for h in range(2):
             gather("V", T.xx, T.w0[:, 0:V], T.sf, 64 * h, 64 * h + 32, w0k, "x%d" % (2 * h))
             gather("S", T.xx, T.w0[:, 0:V], T.sf, 64 * h + 32, 64 * h + 64, w0k, "x%d" % (2 * h + 1))
-            mm(tolist(T.pe, T.xx, "e23", 64 * h, 64 * h + 64, True, True), ["x%d" % (2 * h), "x%d" % (2 * h + 1), "e23"], ["PE"])
-        scp(T.dfa[:], turned[0], [], ["dfa"], ["D0"])
-        cp(T.f2u[:], T.pe[:, 0:128], [], ["f2u"], ["PE"])
-        xk = ["x0", "x1", "x2", "x3", "f2u"]
-        if t == 0:
-            op("S", lambda: act.activation(T.kcol[:], T.k16[:], ACT.Identity, bias=T.rcol[:, 1:2]), ["k16", "rhalf"], ["kcol"])
-        gather("V", T.yy, T.xx[:, 0:V], T.f2u, 0, 64, xk, "y0")
-        gather("S", T.yy, T.xx[:, 0:V], T.f2u, 64, 128, xk, "y1")
-        yk = ["y0", "y1", "f2u"]
-        mm([(T.pd[:, 512 + r:640:16], T.yy[:, r::16], T.e56[:, 8:16], False, r == 15) for r in range(16)], ["y0", "y1", "e56"], ["D1"])
+            mm(tolist(f2p[h][1], T.xx, "e23", 64 * h, 64 * h + 64, True, True), ["x%d" % (2 * h), "x%d" % (2 * h + 1), "e23"],
+               [f2p[h][0]])
+        for h in range(2):
+            cp(T.f2u[:, 64 * h:64 * h + 64], f2p[h][1][:, 64 * h:64 * h + 64], [], ["f2%d" % h], [f2p[h][0]])
+            xk = ["x0", "x1", "x2", "x3", "f2%d" % h]
+            gather("V", T.yy, T.xx[:, 0:V], T.f2u, 64 * h, 64 * h + 32, xk, "y%d" % (2 * h))
+            gather("S", T.yy, T.xx[:, 0:V], T.f2u, 64 * h + 32, 64 * h + 64, xk, "y%d" % (2 * h + 1))
+        yk = ["y0", "y1", "y2", "y3", "f20", "f21"]
+        mm([(T.pd[:, 512 + r:640:16], T.yy[:, r::16], T.e56[:, 8:16], False, r == 15) for r in range(16)], yk[:4] + ["e56"], ["D1"])
         gather("V", T.zz, T.yy[:, 0:V], T.f2u, 0, 64, yk, "c0")
         gather("S", T.zz, T.yy[:, 0:V], T.f2u, 64, 128, yk, "c1")
         mm([(T.pd[:, 1024 + r:1280:16], T.zz[:, r::16], T.e56[:], False, r == 15) for r in range(16)], ["c0", "c1"], ["D2"])
+        if t == 0:
+            op("S", lambda: act.activation(T.kcol[:], T.k16[:], ACT.Identity, bias=T.rcol[:, 1:2]), ["k16", "rhalf"], ["kcol"])
         tt(T.p4[:], turned[1], T.dfa[:], ALU.mult, ["dfa"], ["p4"], ["D1"])
         tt(T.p5[:], turned[2], T.p4[:], ALU.mult, ["p4"], ["p5"], ["D2"])
-        tt(T.p6[:], turned[3], T.p5[:], ALU.mult, ["p5"], ["p6"], ["D2"])
-        ts(T.ut[:], T.p6[:], 0.0, None, ALU.not_equal, None, ["p6"], ["ut"])
+        tt(T.ut[:], turned[3], T.p5[:], ALU.mult, ["p5"], ["ut"], ["D2"])
         mm([(T.pe[:, 0:128], T.ut[:], T.eye[:], True, True)], ["ut"], ["PE"])
-        cp(T.ub[:, 0:128], T.pe[:, 0:128], [], ["ub"], ["PE"])
+        ts(T.ub[:, 0:128], T.pe[:, 0:128], 0.0, None, ALU.not_equal, None, [], ["ub"], ["PE"])
         ts(T.ub[:, 128:NB], T.pe[:, 0:NB - 128], 0.0, None, ALU.is_equal, None, [], ["ue"], ["PE"])
         mm([(T.pd[:, 1536:1536 + NB], T.bo[:], T.ub[:, 0:NB], True, True),
             (T.pd[:, 1792:1792 + NB], T.nsu[:], T.ub[:, 0:NB], True, True)], ["ub", "ue", "bo", "nsu"], ["D3"])
         tt(T.tt[:], T.pb[:, 0:128], T.ub[:, 0:128], ALU.mult, ["ub"], ["tt"], ["PB"])
+        tt(T.ss[:], T.pb[:, 128:256], T.tt[:], ALU.subtract, ["tt"], ["ss"], ["PB"])
         op("V", lambda: vec.tensor_tensor_scan(T.bb[:, 0:NB], T.pd[:, 1536:1536 + NB], T.c255[:, 0:NB], 0.0, ALU.add, ALU.min),
            ["c255"], ["bb"], ["D3"])
         for j in range(NVJ, 12):
             op("S", lambda j=j: act.activation(T.junk[:, NB * (j - NVJ):NB * (j - NVJ + 1)], T.bb[:, 0:NB], ACT.Sign,
                                                bias=T.kcol[:, j:j + 1], scale=-1.0, accum_out=T.acc[:, j:j + 1]),
                ["bb", "kcol"], ["acc%d" % j])
+        cp(su[:], T.ss[:], ["ss"], ["su%d" % t])
+        send(to, ls[:, 0:12], su[:, 0:12], "as%d" % t, ["su%d" % t])
         for j in range(NVJ):
             ts(T.fl[:, NB * j:NB * (j + 1)], T.bb[:, 0:NB], T.kcol[:, j:j + 1], None, ALU.is_le, None, ["bb", "kcol"], ["fl%d" % j])
         op("V", lambda: vec.tensor_tensor_scan(T.fs[:], T.rst[:], T.fl[:], 0.0, ALU.mult, ALU.add),
@@ -353,16 +357,13 @@ def rank_program(g, core, T, topo):
         tt(T.cmp[:], T.cuml[:, 0:NB].indirect(T.cu[:, 0:12]), T.kw[:], ALU.is_le, ["cuml", "cua", "cub", "kw"], ["cmp"])
         mm([(T.pe[:, 0:12], T.eye16[:], T.cb[:, 0:12], True, False)] + tolist(T.pe, T.cmp, "e1", 0, 12, False, True),
            ["cba", "cbb", "cmp", "e1"], ["PE"])
-        tt(T.ss[:], T.pb[:, 128:256], T.tt[:], ALU.subtract, ["tt"], ["ss"], ["PB"])
-        cp(su[:], T.ss[:], ["ss"], ["su%d" % t])
-        send(to, ls[:, 0:12], su[:, 0:12], "as%d" % t, ["su%d" % t])
+        gather("S", zn, zw, su, 0, ZS, [zk, "su%d" % t], znk + "a")
+        gather("V", zn, zw, su, ZS, 128, [zk, "su%d" % t], znk + "b")
         cp(vu[:, 0:12], T.pe[:, 0:12], [], ["vu%d" % t], ["PE"])
         send(to, lv[:, 0:12], vu[:, 0:12], "av%d" % t, ["vu%d" % t])
-        gather("S", zn, zw, su, 0, ZS, [zk, "su%d" % t], znk + "a")
         cp(T.vi[:, 0:12], T.pe[:, 0:12], [], ["vi"], ["PE"])
         ts(T.oi[:, 0:12], T.vi[:, 0:12], V - 1, None, ALU.bitwise_and, None, ["vi"], ["oi"])
         cp(T.ou[:, 0:12], T.oi[:, 0:12], ["oi"], ["ou"])
-        gather("V", zn, zw, su, ZS, 128, [zk, "su%d" % t], znk + "b")
         if t + 1 < RO:
             preload()
             wish_sums()

from concourse.mybir import AluOpType, ActivationFunctionType

ALU = AluOpType
ACT = ActivationFunctionType
V, CAP, RO, N = 2048, 192, 2, 8
NB = 140
BF, F32, I32, U16 = "bfloat16", "float32", "int32", "uint16"
NVJ = 5
ZS = 108

SCRATCH = {"q2": ("sbuf", [128, 8, 16, 16], BF), "pd": ("psum", [128, 2048], F32)}
for _dt, _n, _names in (
        (BF, V, "w z0 z1 z2 m0 m1 m2 m3 mo zg3 w0 xx yy zz"), (BF, V + CAP, "r0 r1"), (BF, 512, "cflag chi clo zg2"),
        (BF, 128, "ones eye neye eye16 eye128 eye2k bo nsu a16 alo lob hib ut"), (BF, 16, "blk nblk cb e56"),
        (BF, 256, "neye2"), (BF, 144, "e23 e1 c255 ub bb cuml"), (BF, 640, "cc"), (BF, CAP, "kw cmp inc"),
        (BF, NB * NVJ, "rst fl fs"), (BF, NB * (12 - NVJ), "junk"),
        (F32, 128, "bst dfa p4 p5 tt ss"), (F32, 16, "rcol k16 kcol acc"),
        (I32, 512, "candi"), (I32, 128, "besti loi hii"), (I32, 16, "pint rint vi oi"),
        (U16, 512, "candu"), (U16, 128, "su0 su1 sf f2u"), (U16, 16, "ls0 ls1 lv0 lv1 vu0 vu1 cu ou")):
    for _name in _names.split():
        SCRATCH[_name] = ("sbuf", [128, _n], _dt)
for _name in ("pa", "pb", "pc", "pe"):
    SCRATCH[_name] = ("psum", [128, 512], F32)
SEMAPHORES = ["sV", "sS", "sT", "sG", "ldc", "ldz", "ldwa", "ldwb", "sent", "stored",
              "az0", "az1", "as0", "as1", "av0", "av1"]


def rank_program(g, core, T, topo):
    rank = T.rank_of(core)
    if rank is None:
        return
    queue = {"V": g.vector, "S": g.scalar, "T": g.tensor, "G": g, "Y": g.sync}
    count = {"V": 0, "S": 0, "T": 0, "G": 0}
    seen = {e: {} for e in queue}
    writer, readers, bank = {}, {}, {}

    def wait(e, tok):
        if seen[e].get(tok[0], 0) < tok[1]:
            queue[e].wait_ge(T.sem[tok[0]], tok[1])
            seen[e][tok[0]] = tok[1]

    def need(e, rd, wr=(), ps=()):
        toks = [writer[k] for k in rd]
        for k in wr:
            toks += readers.get(k, []) + ([writer[k]] if k in writer else [])
        for k in ps:
            toks += [t for o, t in bank.get(k, {}).items() if o != e]
        best = {}
        for s, n, o in toks:
            if not (e == "T" and o == "T"):
                best[s] = max(best.get(s, 0), n)
        for s, n in best.items():
            wait(e, (s, n))

    def op(e, fn, rd=(), wr=(), ps=()):
        need(e, rd, wr, ps)
        fn().then_inc(T.sem["s" + e], 1)
        count[e] += 1
        tok = ("s" + e, count[e], e)
        for k in rd:
            readers.setdefault(k, []).append(tok)
        for k in wr:
            writer[k] = tok
            readers[k] = []
        for k in ps:
            bank.setdefault(k, {})[e] = tok

    def mm(items, rd, ps):
        def run():
            last = None
            for o, l, r, a, b in items:
                last = g.tensor.matmul(o, l, r, a, b)
            return last
        op("T", run, rd, (), ps)

    vec, act = g.vector, g.scalar

    def ts(o, i, s1, s2, o0, o1, rd, wr, ps=()):
        if s2 is None:
            op("V", lambda: vec.tensor_scalar(o, i, s1, None, o0), rd, wr, ps)
        else:
            op("V", lambda: vec.tensor_scalar(o, i, s1, s2, o0, o1), rd, wr, ps)

    def tt(o, a, b, alu, rd, wr, ps=()):
        op("V", lambda: vec.tensor_tensor(o, a, b, alu), rd, wr, ps)

    def cp(o, i, rd, wr, ps=()):
        op("V", lambda: vec.tensor_copy(o, i), rd, wr, ps)

    def scp(o, i, rd, wr, ps=(), fn=ACT.Copy):
        op("S", lambda: act.activation(o, i, fn), rd, wr, ps)

    def iota(o, pat, base, ch, wr, small=True):
        if small:
            op("G", lambda: g.iota(o, pat, base, ch, allow_small_or_imprecise_dtypes=True), (), wr)
        else:
            op("G", lambda: g.iota(o, pat, base, ch), (), wr)

    def sel(o, i, pat, alu, fill, base, ch, rd, wr):
        op("G", lambda: g.affine_select(o, i, pat, alu, fill, base, ch), rd, wr)

    nsent = [0]

    def send(dst, o, i, sem, rd):
        d = T.cores[dst]
        rid, pid = topo.addr(d, core)
        need("G", rd)
        g.remote_dma(o, i, T.sem[sem], T.sem.sent, pid, rid, topo.mask(core, d))
        nsent[0] += len(topo.engines(core, d))

    g.sync.dma_start(T.candi[:], T.cand[:]).then_inc(T.sem.ldc, 16)
    g.scalar.dma_start(T.z0[:], T.goods[:]).then_inc(T.sem.ldz, 16)
    g.sync.dma_start(T.w[:, 0:1024], T.wish[:, 0:1024]).then_inc(T.sem.ldwa, 16)
    g.sync.dma_start(T.w[:, 1024:V], T.wish[:, 1024:V]).then_inc(T.sem.ldwb, 16)
    writer["candi"], writer["z0"] = ("ldc", 16, ""), ("ldz", 16, "")
    writer["wa"], writer["wb"] = ("ldwa", 16, ""), ("ldwb", 16, "")
    for t in range(RO):
        n = len(topo.engines(T.cores[(rank - 1 - t) % N], core))
        writer["r%d" % t], writer["ls%d" % t], writer["lv%d" % t] = ("az%d" % t, n, ""), ("as%d" % t, n, ""), ("av%d" % t, n, "")

    def wk(a0, a1):
        return (["wa"] if a0 < 1024 else []) + (["wb"] if a1 > 1024 else [])

    op("V", lambda: vec.memset(T.ones[:], 1.0), (), ["ones"])
    iota(T.pint[:, 0:1], [[0, 1]], 0, 1, ["pint"], small=False)
    iota(T.a16[:], [[16, 128]], 0, 0, ["a16"])
    sel(T.eye[:], T.ones[:], [[-1, 128]], ALU.is_equal, 0.0, 0, 1, ["ones"], ["eye"])
    sel(T.bo[:], T.ones[:], [[-16, 8], [0, 16]], ALU.is_ge, 0.0, 0, 1, ["ones"], ["bo"])
    sel(T.bo[:], T.bo[:], [[16, 8], [0, 16]], ALU.is_ge, 0.0, 15, -1, ["bo"], ["bo"])
    op("V", lambda: vec.memset(T.cc[0:64, :], -262144.0), (), ["cc0"])
    for j, p in enumerate((4, 0, 3, 2, 1)):
        op("V", lambda j=j, p=p: vec.memset(T.cc[64:128, 128 * j:128 * j + 128], 32.0 * p), (), ["cc%d" % (j + 1)])
    ccs = ["cc%d" % j for j in range(6)]
    ts(T.rint[:, 0:1], T.pint[:, 0:1], 15, None, ALU.bitwise_and, None, ["pint"], ["rint"])
    cp(T.rcol[:, 0:1], T.rint[:, 0:1], ["rint"], ["rcol"])
    ts(T.rcol[:, 1:2], T.rint[:, 0:1], 0.5, None, ALU.add, None, ["rint"], ["rhalf"])
    op("S", lambda: act.activation(T.alo[:], T.ones[:], ACT.Identity, scale=T.rcol[:, 0:1]), ["ones", "rcol"], ["alo"])
    for nm, s in (("neye", -1.0), ("eye2k", 2048.0)):
        op("S", lambda nm=nm, s=s: act.activation(T[nm][:], T.eye[:], ACT.Copy, scale=s), ["eye"], [nm])
    for nm, c, s in (("blk", 0, 8192.0), ("blk", 8, 8192.0), ("nblk", 0, -8192.0)):
        op("S", lambda nm=nm, c=c, s=s: act.activation(T[nm][:, c:c + 8], T.bo[:, 0::16], ACT.Copy, scale=s), ["bo"], [nm])
    for nm, s in (("eye16", 16.0), ("eye128", 128.0)):
        op("S", lambda nm=nm, s=s: act.activation(T[nm][:], T.eye[:], ACT.Copy, scale=s), ["eye"], [nm])
    mm([x for d in range(4) for x in ((T.pe[:, 128 * d:128 * d + 128], T.eye[:], T.a16[:], True, False),
                                      (T.pe[:, 128 * d:128 * d + 128], T.eye[:], T.alo[:], False, True))],
       ["eye", "a16", "alo"], ["PE"])
    cp(T.candu[:], T.candi[:], ["candi"], ["candu"])
    cp(T.chi[:], T.candi[:], ["candi"], ["chi"])
    mm([(T.pc[:], T.eye[:], T.chi[:], True, True)], ["chi"], ["PC"])
    tt(T.cflag[:], T.candi[:], T.pe[:], ALU.is_le, ["candi"], ["cflag"], ["PE"])
    tt(T.clo[:], T.candi[:], T.pc[:], ALU.subtract, ["candi"], ["clo"], ["PC"])

    def later_constants():
        iota(T.q2[:], [[0, 2048]], 0, 0, ["q2"])
        iota(T.q2[:, :, 0, :], [[0, 8], [1, 16]], 0, 0, ["q2"])
        iota(T.q2[:, :, 1, :], [[0, 128]], 0, 1, ["q2"])
        iota(T.e23[:], [[0, 144]], 0, 0, ["e23"])
        iota(T.e56[:], [[0, 16]], 0, 0, ["e56"])
        for nm, col, p in (("e23", T.e23[:, 15:143:16], 2), ("e56", T.e56[:, 0:8], 0), ("e56", T.e56[:, 8:16], 2)):
            sel(col, col, [[-16, 8]], ALU.not_equal, 1.0, -p, 1, [nm], [nm])
            sel(col, col, [[-16, 8]], ALU.not_equal, 16.0, -p - 1, 1, [nm], [nm])
        iota(T.neye2[:], [[0, 256]], -1, 0, ["neye2"])
        sel(T.neye2[:], T.neye2[:], [[0, 2], [-1, 128]], ALU.is_equal, 0.0, 0, 1, ["neye2"], ["neye2"])
        iota(T.e1[:], [[0, 144]], 0, 0, ["e1"])
        sel(T.e1[:, 15:143:16], T.bo[:, 0::16], [[0, 8]], ALU.is_ge, 0.0, 0, 0, ["bo"], ["e1"])
        iota(T.nsu[:], [[0, 128]], -1, 0, ["nsu"])
        sel(T.nsu[:], T.nsu[:], [[-1, 128]], ALU.is_gt, 0.0, 0, 1, ["nsu"], ["nsu"])
        sel(T.nsu[:], T.nsu[:], [[16, 8], [0, 16]], ALU.is_ge, 0.0, 15, -1, ["nsu"], ["nsu"])
        iota(T.kw[:], [[1, CAP]], 0, 0, ["kw"])
        iota(T.c255[:], [[0, 144]], 255, 0, ["c255"])
        iota(T.rst[:], [[0, NB * NVJ]], 1, 0, ["rst"])
        iota(T.rst[:, 0::NB], [[0, NVJ]], 0, 0, ["rst"])
        iota(T.k16[:], [[16, 16]], 0, 0, ["k16"])

    plane = {"o": ("PA", T.pa, 0), 3: ("PA", T.pa, 128), 0: ("PB", T.pb, 0), 1: ("PB", T.pb, 128), 2: ("PC", T.pc, 0)}

    def low(d):
        b, buf, c0 = plane[d]
        o = buf[:, c0:c0 + 128]
        if d == "o":
            return [(o, T.a16[:], T.eye[:], False, False), (o, T.alo[:], T.eye[:], False, False)]
        s = slice(128 * d, 128 * d + 128)
        return [(o, T.cflag[:, s], T.eye2k[:], False, False), (o, T.chi[:, s], T.eye[:], False, False),
                (o, T.clo[:, s], T.eye[:], False, False)]

    lowrd = ["ones", "a16", "alo", "eye", "eye2k", "chi", "clo", "cflag"] + ccs

    def preload():
        mm([(T.pa[:, 0:256], T.ones[:], T.cc[:, 0:256], True, False)] + low("o") + low(3), lowrd, ["PA"])
        mm([(T.pc[:, 0:128], T.ones[:], T.cc[:, 512:640], True, False)] + low(2), lowrd, ["PC"])
        mm([(T.pb[:, 0:256], T.ones[:], T.cc[:, 256:512], True, False)] + low(0) + low(1), lowrd, ["PB"])

    def sums(d, src, w8, c0, c1, rd, stop=False):
        b, buf, o0 = plane[d]
        mm([(buf[c0:c1, o0 + r:o0 + 128:16], src[:, 16 * c0 + r:16 * c1:16], T[w8][:, 0:8], False, stop and r == 15)
            for r in range(16)], rd + [w8], [b])

    def diffs(src, s0, w0, n, b0, rd):
        it = []
        for j in range(n):
            o = T.pd[:, 512 * (b0 + j):512 * (b0 + j + 1)]
            it += [(o, T.eye[:], T.w[:, w0 + 512 * j:w0 + 512 * (j + 1)], True, False),
                   (o, T.neye[:], src[:, s0 + 512 * j:s0 + 512 * (j + 1)], False, True)]
        mm(it, rd + wk(w0, w0 + 512 * n) + ["eye", "neye"], ["D%d" % (b0 + j) for j in range(n)])

    def relu(dst, c0, n, b0, key):
        scp(dst[:, c0:c0 + 512 * n], T.pd[:, 512 * b0:512 * (b0 + n)], [], [key], ["D%d" % (b0 + j) for j in range(n)], ACT.Relu)

    def tolist(out, src, e, c0, c1, first, last):
        return [(out[:, c0:c1], T[e][:, 15 - r:143 - r], src[:, 16 * c0 + r:16 * c1:16], first and r == 0, last and r == 15)
                for r in range(16)]

    def gather(e, dst, win, off, c0, c1, rd, key, d0=0):
        o, i = dst[:, d0 + 16 * c0:d0 + 16 * c1], win.indirect(off[:, c0:c1])
        if e == "V":
            cp(o, i, rd, [key])
        else:
            scp(o, i, rd, [key])

    ww = ["wa", "wb"]

    def wish_sums():
        mm([(T.pa[:, r:256:16], T.w[:, r::16], T.blk[:], False, False) for r in range(16)], ww + ["blk"], ["PA"])
        sums(2, T.w, "blk", 96, 128, ww)

    zbuf = [T.z0, T.z1, T.z2]
    for t in range(RO):
        z, zn, zk, znk = zbuf[t], zbuf[t + 1], "z%d" % t, "z%d" % (t + 1)
        to = (rank + 1 + t) % N
        rwin, su, vu, ls, lv = T["r%d" % t], T["su%d" % t], T["vu%d" % t], T["ls%d" % t], T["lv%d" % t]
        zw = z[:, 0:V]
        send(to, rwin[:, 0:V], z[:, 0:V], "az%d" % t, [zk] + ww)
        if t == 0:
            later_constants()

        def gmin(d, c0, c1, key):
            tt(T["m%d" % d][:, 16 * c0:16 * c1], zw.indirect(T.candu[:, 128 * d + c0:128 * d + c1]), T.w[:, 16 * c0:16 * c1],
               ALU.min, [zk, "candu"] + wk(16 * c0, 16 * c1), [key])

        def gsc(dst, d, c0, c1, o0, key):
            scp(dst[:, o0:o0 + 16 * (c1 - c0)], zw.indirect(T.candu[:, 128 * d + c0:128 * d + c1]), [zk, "candu"], [key])

        if t == 0:
            gmin(0, 0, 64, "m0a")
            gmin(0, 64, 128, "m0")
        else:
            need("V", [], ["m0a"])
            gmin(0, 0, 128, "m0")
        gsc(T.zg3, 3, 0, 128, 0, "g3")
        if t == 0:
            preload()
        diffs(z, 0, 0, 2, 0, [zk])
        diffs(z, 1024, 1024, 2, 2, [zk])
        relu(T.mo, 0, 2, 0, "moa")
        sums(0, T.m0, "blk", 0, 128, ["m0a", "m0"])
        diffs(T.zg3, 0, 0, 2, 0, ["g3"])
        relu(T.mo, 1024, 2, 2, "mob")
        gsc(T.zg2, 2, 96, 128, 0, "g2")
        diffs(T.zg3, 1024, 1024, 2, 2, ["g3"])
        relu(T.m3, 0, 2, 0, "m3a")
        gmin(1, 0, 128, "m1")
        gmin(2, 0, 64, "m2a")
        if t == 0:
            wish_sums()
        sums(1, T.m1, "blk", 0, 128, ["m1"], stop=True)
        sums("o", T.mo, "nblk", 0, 128, ["moa", "mob"])
        diffs(T.zg2, 0, 1536, 1, 0, ["g2"])
        relu(T.m3, 1024, 2, 2, "m3b")
        scp(T.bst[:], T.pb[:, 0:128], [], ["bst"], ["PB"])
        gmin(2, 64, 96, "m2b")
        tt(T.bst[:], T.pb[:, 128:256], T.bst[:], ALU.max, ["bst"], ["bst"], ["PB"])
        relu(T.m2, 1536, 1, 0, "m2c")
        sums(2, T.m2, "blk", 0, 64, ["m2a"], stop=True)
        sums(3, T.m3, "nblk", 0, 128, ["m3a", "m3b"], stop=True)
        sums(2, T.m2, "nblk", 96, 128, ["m2c"], stop=True)
        sums(2, T.m2, "blk", 64, 96, ["m2b"], stop=True)
        tt(T.bst[:], T.pa[:, 0:128], T.bst[:], ALU.max, ["bst"], ["bst"], ["PA"])
        tt(T.bst[:], T.pa[:, 128:256], T.bst[:], ALU.max, ["bst"], ["bst"], ["PA"])
        tt(T.besti[:], T.pc[:, 0:128], T.bst[:], ALU.max, ["bst"], ["besti"], ["PC"])
        ts(T.loi[:], T.besti[:], 15, None, ALU.bitwise_and, None, ["besti"], ["loi"])
        ts(T.hii[:], T.besti[:], 4, 127, ALU.arith_shift_right, ALU.bitwise_and, ["besti"], ["hii"])
        need("V", ["q2"])
        cp(T.q2[:, :, 2, :], T.loi[:], ["loi"], ["qlo"])
        cp(T.q2[:, :, 3, :], T.hii[:], ["hii"], ["qhi"])
        q = ["q2", "qlo", "qhi"]
        cp(T.lob[:], T.q2[:, :, 2, :], ["qlo"], ["lob"])
        cp(T.hib[:], T.q2[:, :, 3, :], ["qhi"], ["hib"])
        for b in range(4):
            mm([(T.pd[:, 128 * r:128 * r + 128], T.q2[:, :, :, r], T.eye[:], True, True) for r in range(4 * b, 4 * b + 4)],
               q, ["D%d" % b])
            if b == 0:
                mm([(T.pe[:, 0:128], T.lob[:], T.eye128[:], True, False),
                    (T.pe[:, 0:128], T.hib[:], T.eye[:], False, True)], ["lob", "hib", "eye128"], ["PE"])
        turned = [T.pc[:, 0:128], T.pd[:, 512:640], T.pd[:, 1024:1152], T.pd[:, 1152:1280]]
        mm([(turned[0], T.eye[:], T.lob[:], True, False), (turned[0], T.eye16[:], T.hib[:], False, False),
            (turned[0], T.a16[:], T.neye[:], False, False), (turned[0], T.alo[:], T.neye[:], False, True)], ["eye16"], ["PC"])
        mm([(T.pb[:, 128:256], T.lob[:], T.eye[:], True, False),
            (T.pb[:, 128:256], T.hib[:], T.eye16[:], False, True),
            (T.pb[:, 0:128], T.lob[:], T.eye[:], True, False),
            (T.pb[:, 0:128], T.hib[:], T.eye16[:], False, False),
            (T.pb[:, 0:128], T.neye[:], T.a16[:], False, False),
            (T.pb[:, 0:128], T.neye[:], T.alo[:], False, True)], ["lob", "hib"], ["PB"])
        cp(T.sf[:], T.pe[:, 0:128], [], ["sf"], ["PE"])
        for b in range(4):
            (scp if b % 2 == 0 else cp)(T.w0[:, 512 * b:512 * b + 512], T.pd[:, 512 * b:512 * b + 512], [], ["w0%d" % b], ["D%d" % b])
        scp(T.dfa[:], turned[0], [], ["dfa"], ["PC"])
        mm([(turned[1], T.a16[:], T.neye[:], True, False), (turned[1], T.alo[:], T.neye[:], False, False)], [], ["D1"])
        mm([(T.pd[:, 1024:1280], T.a16[:], T.neye2[:], True, False), (T.pd[:, 1024:1280], T.alo[:], T.neye2[:], False, False)],
           ["neye2"], ["D2"])
        w0k = ["w0%d" % b for b in range(4)] + ["sf"]
        f2p = [("PE", T.pe), ("PA", T.pa)]
        for h in range(2):
            gather("V", T.xx, T.w0[:, 0:V], T.sf, 64 * h, 64 * h + 32, w0k, "x%d" % (2 * h))
            gather("S", T.xx, T.w0[:, 0:V], T.sf, 64 * h + 32, 64 * h + 64, w0k, "x%d" % (2 * h + 1))
            mm(tolist(f2p[h][1], T.xx, "e23", 64 * h, 64 * h + 64, True, True), ["x%d" % (2 * h), "x%d" % (2 * h + 1), "e23"],
               [f2p[h][0]])
        for h in range(2):
            cp(T.f2u[:, 64 * h:64 * h + 64], f2p[h][1][:, 64 * h:64 * h + 64], [], ["f2%d" % h], [f2p[h][0]])
            xk = ["x0", "x1", "x2", "x3", "f2%d" % h]
            gather("V", T.yy, T.xx[:, 0:V], T.f2u, 64 * h, 64 * h + 32, xk, "y%d" % (2 * h))
            gather("S", T.yy, T.xx[:, 0:V], T.f2u, 64 * h + 32, 64 * h + 64, xk, "y%d" % (2 * h + 1))
        yk = ["y0", "y1", "y2", "y3", "f20", "f21"]
        mm([(T.pd[:, 512 + r:640:16], T.yy[:, r::16], T.e56[:, 8:16], False, r == 15) for r in range(16)], yk[:4] + ["e56"], ["D1"])
        gather("V", T.zz, T.yy[:, 0:V], T.f2u, 0, 64, yk, "c0")
        gather("S", T.zz, T.yy[:, 0:V], T.f2u, 64, 128, yk, "c1")
        mm([(T.pd[:, 1024 + r:1280:16], T.zz[:, r::16], T.e56[:], False, r == 15) for r in range(16)], ["c0", "c1"], ["D2"])
        if t == 0:
            op("S", lambda: act.activation(T.kcol[:], T.k16[:], ACT.Identity, bias=T.rcol[:, 1:2]), ["k16", "rhalf"], ["kcol"])
        tt(T.p4[:], turned[1], T.dfa[:], ALU.mult, ["dfa"], ["p4"], ["D1"])
        tt(T.p5[:], turned[2], T.p4[:], ALU.mult, ["p4"], ["p5"], ["D2"])
        tt(T.ut[:], turned[3], T.p5[:], ALU.mult, ["p5"], ["ut"], ["D2"])
        mm([(T.pe[:, 0:128], T.ut[:], T.eye[:], True, True)], ["ut"], ["PE"])
        ts(T.ub[:, 0:128], T.pe[:, 0:128], 0.0, None, ALU.not_equal, None, [], ["ub"], ["PE"])
        ts(T.ub[:, 128:NB], T.pe[:, 0:NB - 128], 0.0, None, ALU.is_equal, None, [], ["ue"], ["PE"])
        mm([(T.pd[:, 1536:1536 + NB], T.bo[:], T.ub[:, 0:NB], True, True),
            (T.pd[:, 1792:1792 + NB], T.nsu[:], T.ub[:, 0:NB], True, True)], ["ub", "ue", "bo", "nsu"], ["D3"])
        tt(T.tt[:], T.pb[:, 0:128], T.ub[:, 0:128], ALU.mult, ["ub"], ["tt"], ["PB"])
        tt(T.ss[:], T.pb[:, 128:256], T.tt[:], ALU.subtract, ["tt"], ["ss"], ["PB"])
        op("V", lambda: vec.tensor_tensor_scan(T.bb[:, 0:NB], T.pd[:, 1536:1536 + NB], T.c255[:, 0:NB], 0.0, ALU.add, ALU.min),
           ["c255"], ["bb"], ["D3"])
        for j in range(NVJ, 12):
            op("S", lambda j=j: act.activation(T.junk[:, NB * (j - NVJ):NB * (j - NVJ + 1)], T.bb[:, 0:NB], ACT.Sign,
                                               bias=T.kcol[:, j:j + 1], scale=-1.0, accum_out=T.acc[:, j:j + 1]),
               ["bb", "kcol"], ["acc%d" % j])
        cp(su[:], T.ss[:], ["ss"], ["su%d" % t])
        send(to, ls[:, 0:12], su[:, 0:12], "as%d" % t, ["su%d" % t])
        for j in range(NVJ):
            ts(T.fl[:, NB * j:NB * (j + 1)], T.bb[:, 0:NB], T.kcol[:, j:j + 1], None, ALU.is_le, None, ["bb", "kcol"], ["fl%d" % j])
        op("V", lambda: vec.tensor_tensor_scan(T.fs[:], T.rst[:], T.fl[:], 0.0, ALU.mult, ALU.add),
           ["rst"] + ["fl%d" % j for j in range(NVJ)], ["fs"])
        tt(T.cuml[:, 0:NB], T.pd[:, 1792:1792 + NB], T.bb[:, 0:NB], ALU.add, ["bb"], ["cuml"], ["D3"])
        acck = ["acc%d" % j for j in range(NVJ, 12)]
        cp(T.cu[:, 0:NVJ], T.fs[:, NB - 1::NB], ["fs"], ["cua"])
        ts(T.cu[:, NVJ:12], T.acc[:, NVJ:12], 0.5, NB / 2.0, ALU.mult, ALU.add, acck, ["cub"])
        scp(T.cb[:, 0:NVJ], T.fs[:, NB - 1::NB], ["fs"], ["cba"])
        op("S", lambda: act.activation(T.cb[:, NVJ:12], T.acc[:, NVJ:12], ACT.Copy, bias=NB / 2.0, scale=0.5), acck, ["cbb"])
        tt(T.cmp[:], T.cuml[:, 0:NB].indirect(T.cu[:, 0:12]), T.kw[:], ALU.is_le, ["cuml", "cua", "cub", "kw"], ["cmp"])
        mm([(T.pe[:, 0:12], T.eye16[:], T.cb[:, 0:12], True, False)] + tolist(T.pe, T.cmp, "e1", 0, 12, False, True),
           ["cba", "cbb", "cmp", "e1"], ["PE"])
        gather("S", zn, zw, su, 0, ZS, [zk, "su%d" % t], znk + "a")
        gather("V", zn, zw, su, ZS, 128, [zk, "su%d" % t], znk + "b")
        cp(vu[:, 0:12], T.pe[:, 0:12], [], ["vu%d" % t], ["PE"])
        send(to, lv[:, 0:12], vu[:, 0:12], "av%d" % t, ["vu%d" % t])
        cp(T.vi[:, 0:12], T.pe[:, 0:12], [], ["vi"], ["PE"])
        ts(T.oi[:, 0:12], T.vi[:, 0:12], V - 1, None, ALU.bitwise_and, None, ["vi"], ["oi"])
        cp(T.ou[:, 0:12], T.oi[:, 0:12], ["oi"], ["ou"])
        if t + 1 < RO:
            preload()
            wish_sums()
        gather("V", rwin, rwin[:, 0:V], ls, 0, 12, ["r%d" % t, "ls%d" % t], "rx%d" % t, d0=V)
        gather("V", T.inc, rwin[:, 0:V + CAP], lv, 0, 12, ["r%d" % t, "rx%d" % t, "lv%d" % t], "inc")
        cp(zn[:, 0:V].indirect(T.ou[:, 0:12]), T.inc[:], ["inc", "ou", znk + "a", znk + "b"], [znk])

    need("Y", ["z%d" % RO])
    g.sync.dma_start(T.y[:], zbuf[RO][:]).then_inc(T.sem.stored, 16)
    for e in ("V", "S", "T", "G"):
        wait("G", ("s" + e, count[e]))
    g.wait_ge(T.sem.sent, nsent[0])
    g.wait_ge(T.sem.stored, 16)
